import numpy as np
import ml_dtypes


def mxq(x, axis, fmt="e4m3"):
    dtype, down = {"e4m3": (ml_dtypes.float8_e4m3fn, 7), "e5m2": (ml_dtypes.float8_e5m2, 14)}[fmt]
    v = np.moveaxis(np.asarray(x, np.float32).astype(ml_dtypes.bfloat16).astype(np.float64), axis, -1)
    blocks = v.reshape(v.shape[:-1] + (-1, 32))
    amax = np.abs(blocks).max(-1, keepdims=True)
    byte = np.maximum(np.where(amax > 0, np.frexp(amax)[1] - 1 + 127, 0) - down, 1)
    scale = np.exp2(byte - 127.0)
    codes = (blocks / scale).astype(np.float32).astype(dtype).astype(np.float64)
    return np.moveaxis((codes * scale).reshape(v.shape), -1, axis)


WIDE = False


def mx_kscale(k):
    if not WIDE:
        return np.ones(k)
    levels = np.array([10, -10, 5, -5, 0])
    if k % 512:
        return np.exp2(np.random.permutation(np.resize(levels, k // 32))).repeat(32)
    a = np.empty((k // 512, 16))
    for p in range(k // 512):
        a[p, :8] = np.random.permutation(np.resize(levels, 8))
        for g in range(8):
            far = levels[np.abs(levels - a[p, g]) >= 10]
            a[p, g + 8] = far[np.random.randint(len(far))]
    return np.exp2(a.ravel()).repeat(32)


def f64(x):
    return np.asarray(x).astype(np.float64)


def striped(idx):
    return np.tile(idx.reshape(-1, 16).T, (8, 1)).astype(np.uint16)


def unstriped(offs):
    return offs[:16].T.reshape(-1).astype(np.int64)


E2M1 = np.array([0.0, 0.5, 1.0, 1.5, 2.0, 3.0, 4.0, 6.0, -0.0, -0.5, -1.0, -1.5, -2.0, -3.0, -4.0, -6.0])


def pack_weight(w, fmt):
    k, n = w.shape
    w = f64(np.asarray(w, np.float32).astype(ml_dtypes.bfloat16)).reshape(k // 32, 32, n)
    amax = np.abs(w).max(1)
    if fmt == "e4m3":
        byte = np.frexp(amax)[1] - 1 + 127 - 7
    else:
        mant, ex = np.frexp(amax / 6.0)
        byte = np.where(mant > 0.5, ex, ex - 1) + 127
    byte = np.clip(np.where(amax > 0, byte, 1), 1, 254)
    scaled = (w * np.exp2(127.0 - byte)[:, None, :]).reshape(k, n).astype(np.float32)
    by_word = np.ascontiguousarray(scaled.reshape(k // 512, 128, 4, n).transpose(0, 1, 3, 2))
    if fmt == "e4m3":
        words = by_word.astype(ml_dtypes.float8_e4m3fn).view(np.uint8)
    else:
        c = by_word.astype(ml_dtypes.float4_e2m1fn).view(np.uint8) & 0xF
        words = (c[..., 0::2] | (c[..., 1::2] << 4)).reshape(k // 512, 128, 2 * n)
    return np.ascontiguousarray(words), np.ascontiguousarray(byte.astype(np.uint8).reshape(k // 512, 16, n))


def unpack_weight(words, scales, fmt):
    g, _, n = scales.shape
    words = np.ascontiguousarray(words).reshape(g, 128, n, -1)
    if fmt == "e4m3":
        vals = words.view(ml_dtypes.float8_e4m3fn).astype(np.float64)
    else:
        nib = np.empty((g, 128, n, 4), np.uint8)
        nib[..., 0::2] = words & 0xF
        nib[..., 1::2] = words >> 4
        vals = E2M1[nib]
    vals = vals * np.repeat(np.exp2(scales.astype(np.float64) - 127.0), 8, axis=1)[..., None]
    return vals.transpose(0, 1, 3, 2).reshape(g * 512, n)


def gelu(v):
    return 0.5 * v * (1.0 + np.tanh(np.sqrt(2.0 / np.pi) * (v + 0.044715 * v**3)))


def striped8(idx):
    return np.concatenate([v.reshape(-1, 16).T for v in idx]).astype(np.uint16)


def unstriped8(offs):
    return np.stack([offs[16 * g:16 * g + 16].T.reshape(-1) for g in range(8)]).astype(np.int64)


def heads(h, wgt, idx8):
    r = np.arange(h.shape[0])
    return wgt[r // 4 % 128] * h[r[:, None], idx8[r % 512 // 64]]


def put_heads(h, wgs, idx8, t2):
    r = np.arange(h.shape[0])
    page = np.zeros((h.shape[0], t2))
    page[r[:, None], idx8[r % 512 // 64]] = wgs[r // 4 % 128] * h
    return page


K, H, N, T, S, T2, P = 1536, 1024, 256, 2048, 512, 1024, 512


def setup_inputs():
    n = np.random.standard_normal
    s = mx_kscale(K)[:, None]
    u = mx_kscale(H)[:, None]
    d = {}
    d["tab_words"], d["tab_scales"] = pack_weight(n((K, T)) * s, "e4m3")
    d["offs"] = striped(np.random.permutation(T)[:S])
    d["w1"] = (n((K, H)) / K ** 0.5 / s).astype(np.float32)
    d["offs2"] = striped8(np.stack([np.random.permutation(T2)[:S] for _ in range(8)]))
    d["wgs"] = np.repeat(np.random.uniform(0.5, 2.0, (8, S)), 16, axis=0).astype(np.float32)
    d["offs3"] = striped8(np.stack([np.random.permutation(T2)[:P] for _ in range(8)]))
    d["wgt"] = np.repeat(np.random.uniform(0.5, 2.0, (8, P)), 16, axis=0).astype(np.float32)
    d["flow"] = (0.7 + n((H, P))).astype(np.float32)
    d["gact"] = (np.exp(0.3 * n(H)) * u[:, 0]).astype(np.float32)
    d["w2_words"], d["w2_scales"] = pack_weight(1.5 * n((H, H)) / H ** 0.5 / u, "e2m1")
    d["gsum"] = (np.exp(0.3 * n(H)) * u[:, 0]).astype(np.float32)
    d["w3"] = (n((H, N)) / H ** 0.5 / u).astype(np.float32)
    return d


def reference(tab_words, tab_scales, offs, w1, offs2, wgs, offs3, wgt, flow, gact, w2_words, w2_scales, gsum, w3):
    v = unpack_weight(tab_words, tab_scales, "e4m3")[:, unstriped(offs)]
    w2 = unpack_weight(w2_words, w2_scales, "e2m1")
    h = np.abs(mxq(f64(w1), 0, "e4m3").T @ v)
    page = put_heads(h, f64(wgs), unstriped8(offs2), T2)
    diff = heads(page, f64(wgt), unstriped8(offs3)) - f64(flow)
    act = 0.5 * diff * (1.0 + np.tanh(0.7978845608028654 * (diff + 0.044715 * diff ** 3)))
    z = act * f64(gact)[:, None]
    resp = np.tanh(w2.T @ mxq(z, 0, "e4m3"))
    y = (resp + diff) * f64(gsum)[:, None]
    return mxq(f64(w3), 0, "e4m3").T @ mxq(y, 0, "e4m3")

@@ -1,0 +1,338 @@
+from contextlib import ExitStack
+
+import concourse.mybir as mybir
+
+K, H, N, T, S, T2 = 1536, 1024, 256, 2048, 512, 1024
+FLOPS = 2 * K * H * S + 2 * H * H * S + 2 * H * N * S
+
+F32 = mybir.dt.float32
+BF16 = mybir.dt.bfloat16
+I32 = mybir.dt.int32
+U32 = mybir.dt.uint32
+U16 = mybir.dt.uint16
+U8 = mybir.dt.uint8
+FP8X4 = mybir.dt.float8_e4m3fn_x4
+FP4X4 = mybir.dt.float4_e2m1fn_x4
+ACT = mybir.ActivationFunctionType
+ALU = mybir.AluOpType
+
+P = 128
+PACK = 4
+K_PASS = P * PACK
+K_PASSES = K // K_PASS
+H_PASSES = H // K_PASS
+SLICES = H // P
+CHUNKS = 2
+CW = S // CHUNKS
+PAGES = 2
+
+
+def tile_list_perfusion_viability_scores_kernel(
+    tc, tab_words, tab_scales, offs, w1, offs2, wgs, offs3, wgt, flow, gact, w2_words, w2_scales, gsum, w3, out
+):
+    nc = tc.nc
+    with ExitStack() as ctx:
+        keep = ctx.enter_context(tc.tile_pool(name="keep", bufs=1))
+        ring = ctx.enter_context(tc.tile_pool(name="ring", bufs=3))
+        psum = ctx.enter_context(tc.psum_pool(name="psum", bufs=1))
+
+        def held(shape, dtype, name, tag=""):
+            return keep.tile(shape, dtype, name=name, tag=tag or name, align_bytes=64)
+
+        def bank(k, shape, name):
+            return psum.tile(shape, F32, name=name, tag="bank%d" % k)
+
+        list1 = held([P, S // 16], U16, "list1")
+        list2 = held([P, S // 16], U16, "list2")
+        list3 = held([P, S // 16], U16, "list3")
+        tab_planes = held([P, T], U8, "tab_planes")
+        w2_planes_raw = held([P, H_PASSES, H], U8, "w2_planes_raw")
+        nc.vector.memset(tab_planes[:].bitcast(I32), 0)
+        nc.vector.memset(w2_planes_raw[:].rearrange("p a c -> p (a c)").bitcast(I32), 0)
+        pages = [held([P, T2], F32, "page%d" % k) for k in range(PAGES)]
+        for page in pages:
+            nc.vector.memset(page[:], 0.0)
+        for q in range(4):
+            nc.gpsimd.dma_start(
+                out=w2_planes_raw[32 * q : 32 * q + 4, :, :].bitcast(I32),
+                in_=w2_scales[:, 4 * q : 4 * q + 4, :].rearrange("a r c -> r a c").bitcast(I32),
+            )
+
+        w1_slot = {(0, 0): 0, (0, 1): 1, (0, 2): 2, (1, 0): 2, (1, 1): 3, (1, 2): 0}
+        tab_slot = [3, 0, 1]
+        flow_slot = [4, 3]
+        w1_raw, tab = {}, {}
+
+        def load_w1(b, a):
+            w1_raw[b, a] = held([P, PACK, K_PASS], F32, "w1_raw%d%d" % (b, a), tag="big%d" % w1_slot[b, a])
+            rows = w1[a * K_PASS : (a + 1) * K_PASS, b * K_PASS : (b + 1) * K_PASS]
+            nc.sync.dma_start(out=w1_raw[b, a][:], in_=rows.rearrange("(p t) c -> p t c", t=PACK))
+
+        def load_tab(a):
+            tab[a] = held([P, T], I32, "tab%d" % a, tag="big%d" % tab_slot[a])
+            nc.sync.dma_start(out=tab[a][:], in_=tab_words[a].rearrange("p t i -> p (t i)").bitcast(I32))
+
+        load_w1(0, 0)
+        nc.sync.dma_start(list1[:], offs)
+        nc.sync.dma_start(list2[:], offs2)
+        nc.sync.dma_start(list3[:], offs3)
+        load_w1(0, 1)
+        load_w1(0, 2)
+        load_tab(0)
+        for q in range(4):
+            nc.sync.dma_start(
+                out=tab_planes[32 * q : 32 * q + 4 * K_PASSES, :].bitcast(I32),
+                in_=tab_scales[:, 4 * q : 4 * q + 4, :].bitcast(I32),
+            )
+
+        w1_codes, w1_planes = {}, {}
+
+        def round_w1(b, a, staged):
+            nc.scalar.copy(
+                out=staged.rearrange("p (i m t) -> p m t i", i=PACK, t=PACK),
+                in_=w1_raw[b, a][:].rearrange("p t (m i) -> p m t i", i=PACK),
+            )
+
+        def quantize(name, staged, words):
+            codes = held([P, words], U32, name + "_codes")
+            plane = held([P, words], U8, name + "_plane")
+            nc.vector.quantize_mx(out=codes[:].bitcast(FP8X4), scales=plane[:], in_=staged)
+            return codes, plane
+
+        v_words = [held([P, S], U32, "v_words%d" % a) for a in range(K_PASSES)]
+        v_planes = held([P, S], U8, "v_planes")
+
+        def look_up(a):
+            nc.vector.tensor_copy(v_words[a][:], tab[a][:].bitcast(U32).indirect(list1[:]))
+
+        def quantize_w1(b, a, tag):
+            staged = held([P, PACK * K_PASS], BF16, "staged%d%d" % (b, a), tag=tag)
+            round_w1(b, a, staged[:])
+            w1_codes[b, a], w1_planes[b, a] = quantize("w1_%d%d" % (b, a), staged[:], K_PASS)
+
+        quantize_w1(0, 0, "mid0")
+        load_tab(1)
+        quantize_w1(0, 1, "mid1")
+        load_tab(2)
+        gains = held([P, 2 * S + 2 * SLICES], F32, "gains", tag="mid1")
+        wgs_sb, wgt_sb = gains[:, :S], gains[:, S : 2 * S]
+        gact_sb = gains[:, 2 * S : 2 * S + SLICES].rearrange("p (b i) -> p b i", i=PACK)
+        gsum_sb = gains[:, 2 * S + SLICES :].rearrange("p (b i) -> p b i", i=PACK)
+        nc.sync.dma_start(out=wgs_sb, in_=wgs)
+        nc.sync.dma_start(out=wgt_sb, in_=wgt)
+        nc.sync.dma_start(out=gact_sb, in_=gact.rearrange("(b p i) -> p b i", p=P, i=PACK))
+        nc.sync.dma_start(out=gsum_sb, in_=gsum.rearrange("(b p i) -> p b i", p=P, i=PACK))
+        nc.vector.tensor_copy(v_planes[:], tab_planes[:].indirect(list1[:]))
+        quantize_w1(0, 2, "big4")
+        load_w1(1, 0)
+        look_up(0)
+        load_w1(1, 1)
+        look_up(1)
+        load_w1(1, 2)
+        look_up(2)
+        w2_planes = held([P, H_PASSES, H], U8, "w2_planes", tag="big1")
+        nc.vector.tensor_copy(
+            out=w2_planes[:].rearrange("p a (b i m) -> p (a b) i m", i=PACK, m=P),
+            in_=w2_planes_raw[:].rearrange("p a (b m i) -> p (a b) i m", i=PACK, m=P),
+        )
+        flow_sb = {}
+
+        def load_flow(b):
+            flow_sb[b] = held([P, PACK, S], F32, "flow%d" % b, tag="big%d" % flow_slot[b])
+            nc.sync.dma_start(out=flow_sb[b][:], in_=flow.rearrange("(b p i) j -> b p i j", p=P, i=PACK)[b])
+
+        load_flow(0)
+
+        h = {}
+
+        def first_product(s):
+            b, i = divmod(s, PACK)
+            acc = bank(0 if s < PACK else s, [P, S], "h_acc%d" % s)
+            cols = slice(i * P, (i + 1) * P)
+            for a in range(K_PASSES):
+                nc.tensor.matmul_mx(
+                    out=acc[:],
+                    lhsT=w1_codes[b, a][:, cols].bitcast(FP8X4),
+                    lhsT_scale=w1_planes[b, a][:, cols],
+                    rhs=v_words[a][:].bitcast(FP8X4),
+                    rhs_scale=v_planes[4 * a : P, :],
+                    start=(a == 0),
+                    stop=(a == K_PASSES - 1),
+                )
+            h[s] = held([P, S], F32, "h%d" % s)
+            nc.scalar.activation(h[s][:], acc[:], ACT.Abs)
+
+        for s in range(PACK):
+            first_product(s)
+
+        x = {}
+
+        def put(s):
+            nc.vector.tensor_tensor(pages[s % PAGES][:].indirect(list2[:]), h[s][:], wgs_sb, ALU.mult)
+
+        def pick(s, dst):
+            x[s] = dst
+            nc.vector.tensor_tensor(dst, pages[s % PAGES][:].indirect(list3[:]), wgt_sb, ALU.mult)
+
+        def ring_x(s):
+            return ring.tile([P, S], F32, name="x%d" % s, tag="x")[:]
+
+        z16 = [held([P, PACK, S], BF16, "z16_%d" % b) for b in range(H_PASSES)]
+
+        def difference(s, cols):
+            b, i = divmod(s, PACK)
+            d = flow_sb[b][:, i, cols]
+            nc.vector.tensor_tensor(d, x[s][:, cols], d, ALU.subtract)
+
+        def activate(s, cols):
+            b, i = divmod(s, PACK)
+            d = flow_sb[b][:, i, cols]
+            act = ring.tile([P, S], F32, name="act%d_%d" % (s, cols.start), tag="act", bufs=2)
+            nc.scalar.activation(act[:, cols], d, ACT.Gelu_apprx_tanh)
+            nc.scalar.activation(z16[b][:, i, cols], act[:, cols], ACT.Copy, scale=gact_sb[:, b, i : i + 1])
+
+        def residual(s, cols):
+            b, i = divmod(s, PACK)
+            d = flow_sb[b][:, i, cols]
+            nc.scalar.activation(d, d, ACT.Copy, scale=gsum_sb[:, b, i : i + 1])
+
+        def weave(engine_copy, dst, rows):
+            engine_copy(
+                out=dst.rearrange("p (c u t) -> p c t u", u=PACK, t=PACK),
+                in_=rows.rearrange("p t (c u) -> p c t u", u=PACK),
+            )
+
+        whole = slice(0, S)
+        chunk_cols = [slice(c * CW, (c + 1) * CW) for c in range(CHUNKS)]
+
+        for s in (0, 1):
+            put(s)
+            pick(s, ring_x(s))
+
+        quantize_w1(1, 0, "mid0")
+        w2_raw = held([P, H_PASSES, 2 * H], U8, "w2_raw", tag="mid0")
+        nc.sync.dma_start(out=w2_raw[:].bitcast(I32), in_=w2_words.rearrange("a p c -> p a c").bitcast(I32))
+        w3_raw = held([P, H_PASSES, PACK, N], F32, "w3_raw", tag="big2")
+        for b in range(H_PASSES):
+            nc.sync.dma_start(
+                out=w3_raw[:, b], in_=w3[b * K_PASS : (b + 1) * K_PASS, :].rearrange("(p t) n -> p t n", t=PACK)
+            )
+        quantize_w1(1, 1, "mid2")
+        load_flow(1)
+        quantize_w1(1, 2, "hold_a")
+        for s in range(PACK, SLICES):
+            first_product(s)
+
+        x23 = held([P, 2, S], F32, "x23", tag="hold_a")
+        for s in (2, 3):
+            put(s)
+            pick(s, x23[:, s - 2, :])
+        for s in range(PACK):
+            difference(s, whole)
+            activate(s, whole)
+            residual(s, whole)
+
+        w2_codes = held([P, H_PASSES, 2 * H], U8, "w2_codes")
+        nc.scalar.copy(
+            out=w2_codes[:].bitcast(U16).rearrange("p a (b i m) -> p (a b) i m", i=PACK, m=P),
+            in_=w2_raw[:].bitcast(U16).rearrange("p a (b m i) -> p (a b) i m", i=PACK, m=P),
+        )
+
+        z_codes, z_planes, acc2 = {}, {}, {}
+
+        def quantize_z(b, c, engine_copy):
+            woven = held([P, PACK * CW], BF16, "z_woven%d%d" % (b, c), tag="hold_z%d%d" % (b, c))
+            weave(engine_copy, woven[:], z16[b][:, :, chunk_cols[c]])
+            z_codes[b, c], z_planes[b, c] = quantize("z%d%d" % (b, c), woven[:], CW)
+
+        def second_product(a, c):
+            for u in range(SLICES // 2):
+                if a == 0:
+                    acc2[c, u] = bank(PACK * c + u, [P, 2, CW], "acc2_%d%d" % (c, u))
+                for e in range(2):
+                    s = 2 * u + e
+                    nc.tensor.matmul_mx(
+                        out=acc2[c, u][:, e, :],
+                        lhsT=w2_codes[:, a, 2 * P * s : 2 * P * (s + 1)].bitcast(FP4X4),
+                        lhsT_scale=w2_planes[:, a, P * s : P * (s + 1)],
+                        rhs=z_codes[a, c][:].bitcast(FP8X4),
+                        rhs_scale=z_planes[a, c][:],
+                        start=(a == 0 and e == 0),
+                        stop=(a == H_PASSES - 1 and e == 1),
+                    )
+
+        w3_staged = held([P, H_PASSES * PACK * N], BF16, "w3_staged", tag="hold_w3")
+        for b in range(H_PASSES):
+            weave(nc.scalar.copy, w3_staged[:, b * PACK * N : (b + 1) * PACK * N], w3_raw[:, b])
+        w3_codes, w3_plane = quantize("w3", w3_staged[:], H_PASSES * N)
+
+        put(4)
+        pick(4, held([P, S], F32, "x4", tag="hold_w3")[:])
+        difference(4, whole)
+        for c in range(CHUNKS):
+            quantize_z(0, c, nc.scalar.copy)
+            second_product(0, c)
+        activate(4, whole)
+        residual(4, whole)
+        for s in (5, 6):
+            put(s)
+            pick(s, held([P, S], F32, "x%d" % s, tag="hold_z0%d" % (s - 5))[:])
+            difference(s, whole)
+            activate(s, whole)
+            residual(s, whole)
+
+        last = SLICES - 1
+        put(last)
+        x[last] = ring_x(last)
+        for c in range(CHUNKS):
+            cols = chunk_cols[c]
+            nc.vector.tensor_tensor(
+                x[last][:, cols],
+                pages[last % PAGES][:].indirect(list3[:, c * CW // 16 : (c + 1) * CW // 16]),
+                wgt_sb[:, cols],
+                ALU.mult,
+            )
+            difference(last, cols)
+            d = flow_sb[1][:, PACK - 1, cols]
+            act = ring.tile([P, CW], F32, name="act_last%d" % c, tag="act", bufs=2)
+            nc.scalar.activation(act[:], d, ACT.Gelu_apprx_tanh)
+            nc.vector.tensor_scalar_mul(z16[1][:, PACK - 1, cols], act[:], gact_sb[:, 1, PACK - 1 : PACK])
+            quantize_z(1, c, nc.vector.tensor_copy)
+            second_product(1, c)
+            residual(last, cols)
+
+        resp = {}
+        for c in range(CHUNKS):
+            for u in range(SLICES // 2):
+                resp[c, u] = ring.tile([P, 2, CW], F32, name="resp%d%d" % (c, u), tag="resp", bufs=6)
+                nc.scalar.activation(resp[c, u][:], acc2[c, u][:], ACT.Tanh)
+
+        for c in range(CHUNKS):
+            cols = chunk_cols[c]
+            y_codes, y_planes = {}, {}
+            for b in range(H_PASSES):
+                y16 = ring.tile([P, PACK, CW], BF16, name="y16_%d%d" % (c, b), tag="y16")
+                for i in range(PACK):
+                    nc.vector.scalar_tensor_tensor(
+                        y16[:, i, :], resp[c, 2 * b + i // 2][:, i % 2, :], gsum_sb[:, b, i : i + 1],
+                        flow_sb[b][:, i, cols], ALU.mult, ALU.add,
+                    )
+                woven = ring.tile([P, PACK * CW], BF16, name="y_woven%d%d" % (c, b), tag="y_woven", align_bytes=64)
+                weave(nc.scalar.copy if b == 0 else nc.vector.tensor_copy, woven[:], y16[:])
+                y_codes[b], y_planes[b] = quantize("y%d%d" % (c, b), woven[:], CW)
+            acc3 = bank(c, [P, N // P, CW], "acc3_%d" % c)
+            for b in range(H_PASSES):
+                for nt in range(N // P):
+                    w_cols = slice(b * N + nt * P, b * N + (nt + 1) * P)
+                    nc.tensor.matmul_mx(
+                        out=acc3[:, nt, :],
+                        lhsT=w3_codes[:, w_cols].bitcast(FP8X4),
+                        lhsT_scale=w3_plane[:, w_cols],
+                        rhs=y_codes[b][:].bitcast(FP8X4),
+                        rhs_scale=y_planes[b][:],
+                        start=(b == 0 and nt == 0),
+                        stop=(b == H_PASSES - 1 and nt == N // P - 1),
+                    )
+            result = ring.tile([P, N // P, CW], F32, name="result%d" % c, tag="result", bufs=2)
+            nc.scalar.copy(out=result[:], in_=acc3[:])
+            nc.sync.dma_start(out=out[:, cols].rearrange("(nt p) j -> p nt j", p=P), in_=result[:])

@@ -24,7 +24,7 @@ H_PASSES = H // K_PASS
 SLICES = H // P
 CHUNKS = 2
 CW = S // CHUNKS
-PAGES = 2
+PAGES = 3
 
 
 def tile_list_perfusion_viability_scores_kernel(
@@ -41,6 +41,10 @@ def tile_list_perfusion_viability_scores_kernel(
 
         def bank(k, shape, name):
             return psum.tile(shape, F32, name=name, tag="bank%d" % k)
+
+        whole = slice(0, S)
+        chunk_cols = [slice(c * CW, (c + 1) * CW) for c in range(CHUNKS)]
+        chunk_entries = [slice(c * CW // 16, (c + 1) * CW // 16) for c in range(CHUNKS)]
 
         list1 = held([P, S // 16], U16, "list1")
         list2 = held([P, S // 16], U16, "list2")
@@ -60,7 +64,7 @@ def tile_list_perfusion_viability_scores_kernel(
 
         w1_slot = {(0, 0): 0, (0, 1): 1, (0, 2): 2, (1, 0): 2, (1, 1): 3, (1, 2): 0}
         tab_slot = [3, 0, 1]
-        flow_slot = [4, 3]
+        flow_slot = [1, 3]
         w1_raw, tab = {}, {}
 
         def load_w1(b, a):
@@ -88,10 +92,13 @@ def tile_list_perfusion_viability_scores_kernel(
         w1_codes, w1_planes = {}, {}
 
         def round_w1(b, a, staged):
-            nc.scalar.copy(
-                out=staged.rearrange("p (i m t) -> p m t i", i=PACK, t=PACK),
-                in_=w1_raw[b, a][:].rearrange("p t (m i) -> p m t i", i=PACK),
-            )
+            dealt = staged.rearrange("p (i m t) -> p m t i", i=PACK, t=PACK)
+            rows = w1_raw[b, a][:].rearrange("p t (m i) -> p m t i", i=PACK)
+            if b == 0:
+                nc.scalar.copy(out=dealt[:, : P // 2], in_=rows[:, : P // 2])
+                nc.vector.tensor_copy(out=dealt[:, P // 2 :], in_=rows[:, P // 2 :])
+            else:
+                nc.scalar.copy(out=dealt, in_=rows)
 
         def quantize(name, staged, words):
             codes = held([P, words], U32, name + "_codes")
@@ -123,18 +130,21 @@ def tile_list_perfusion_viability_scores_kernel(
         nc.sync.dma_start(out=gact_sb, in_=gact.rearrange("(b p i) -> p b i", p=P, i=PACK))
         nc.sync.dma_start(out=gsum_sb, in_=gsum.rearrange("(b p i) -> p b i", p=P, i=PACK))
         nc.vector.tensor_copy(v_planes[:], tab_planes[:].indirect(list1[:]))
-        quantize_w1(0, 2, "big4")
+        quantize_w1(0, 2, "mid3")
+        w2_planes = held([P, H_PASSES, H], U8, "w2_planes", tag="mid3")
+        nc.vector.tensor_copy(
+            out=w2_planes[:].rearrange("p a (b i m) -> p (a b) i m", i=PACK, m=P),
+            in_=w2_planes_raw[:].rearrange("p a (b m i) -> p (a b) i m", i=PACK, m=P),
+        )
         load_w1(1, 0)
         look_up(0)
         load_w1(1, 1)
         look_up(1)
         load_w1(1, 2)
-        look_up(2)
-        w2_planes = held([P, H_PASSES, H], U8, "w2_planes", tag="big1")
-        nc.vector.tensor_copy(
-            out=w2_planes[:].rearrange("p a (b i m) -> p (a b) i m", i=PACK, m=P),
-            in_=w2_planes_raw[:].rearrange("p a (b m i) -> p (a b) i m", i=PACK, m=P),
-        )
+        for c in range(CHUNKS):
+            nc.vector.tensor_copy(
+                v_words[2][:, chunk_cols[c]], tab[2][:].bitcast(U32).indirect(list1[:, chunk_entries[c]])
+            )
         flow_sb = {}
 
         def load_flow(b):
@@ -143,46 +153,48 @@ def tile_list_perfusion_viability_scores_kernel(
 
         load_flow(0)
 
-        h = {}
+        h = {s: held([P, S], F32, "h%d" % s, tag="row%d" % s) for s in range(SLICES)}
 
-        def first_product(s):
+        def first_product(s, k, cols):
             b, i = divmod(s, PACK)
-            acc = bank(0 if s < PACK else s, [P, S], "h_acc%d" % s)
-            cols = slice(i * P, (i + 1) * P)
+            acc = bank(k, [P, cols.stop - cols.start], "h_acc%d_%d" % (s, cols.start))
+            w_cols = slice(i * P, (i + 1) * P)
             for a in range(K_PASSES):
                 nc.tensor.matmul_mx(
                     out=acc[:],
-                    lhsT=w1_codes[b, a][:, cols].bitcast(FP8X4),
-                    lhsT_scale=w1_planes[b, a][:, cols],
-                    rhs=v_words[a][:].bitcast(FP8X4),
-                    rhs_scale=v_planes[4 * a : P, :],
+                    lhsT=w1_codes[b, a][:, w_cols].bitcast(FP8X4),
+                    lhsT_scale=w1_planes[b, a][:, w_cols],
+                    rhs=v_words[a][:, cols].bitcast(FP8X4),
+                    rhs_scale=v_planes[4 * a : P, cols],
                     start=(a == 0),
                     stop=(a == K_PASSES - 1),
                 )
-            h[s] = held([P, S], F32, "h%d" % s)
-            nc.scalar.activation(h[s][:], acc[:], ACT.Abs)
+            nc.scalar.activation(h[s][:, cols], acc[:], ACT.Abs)
 
-        for s in range(PACK):
-            first_product(s)
+        for c in range(CHUNKS):
+            first_product(0, c, chunk_cols[c])
+        for s in range(1, PACK):
+            first_product(s, (s - 1) % 2, whole)
 
-        x = {}
+        x, gained = {}, {}
+
+        def gain(s, engine, tag):
+            gained[s] = held([P, S], F32, "gained%d" % s, tag=tag)
+            engine.tensor_tensor(gained[s][:], h[s][:], wgs_sb, ALU.mult)
 
         def put(s):
-            nc.vector.tensor_tensor(pages[s % PAGES][:].indirect(list2[:]), h[s][:], wgs_sb, ALU.mult)
+            nc.vector.tensor_copy(pages[s % PAGES][:].indirect(list2[:]), gained[s][:])
 
-        def pick(s, dst):
-            x[s] = dst
-            nc.vector.tensor_tensor(dst, pages[s % PAGES][:].indirect(list3[:]), wgt_sb, ALU.mult)
-
-        def ring_x(s):
-            return ring.tile([P, S], F32, name="x%d" % s, tag="x")[:]
+        def pick(s, tag):
+            x[s] = held([P, S], F32, "x%d" % s, tag=tag)
+            nc.vector.tensor_tensor(x[s][:], pages[s % PAGES][:].indirect(list3[:]), wgt_sb, ALU.mult)
 
         z16 = [held([P, PACK, S], BF16, "z16_%d" % b) for b in range(H_PASSES)]
 
-        def difference(s, cols):
+        def difference(s, cols, engine):
             b, i = divmod(s, PACK)
             d = flow_sb[b][:, i, cols]
-            nc.vector.tensor_tensor(d, x[s][:, cols], d, ALU.subtract)
+            engine.tensor_tensor(d, x[s][:, cols], d, ALU.subtract)
 
         def activate(s, cols):
             b, i = divmod(s, PACK)
@@ -202,12 +214,15 @@ def tile_list_perfusion_viability_scores_kernel(
                 in_=rows.rearrange("p t (c u) -> p c t u", u=PACK),
             )
 
-        whole = slice(0, S)
-        chunk_cols = [slice(c * CW, (c + 1) * CW) for c in range(CHUNKS)]
 
-        for s in (0, 1):
-            put(s)
-            pick(s, ring_x(s))
+        for c in range(CHUNKS):
+            cols = chunk_cols[c]
+            nc.vector.tensor_tensor(
+                pages[0][:].indirect(list2[:, chunk_entries[c]]), h[0][:, cols], wgs_sb[:, cols], ALU.mult
+            )
+        gain(1, nc.vector, "gained1")
+        put(1)
+        gain(2, nc.gpsimd, "row1")
 
         quantize_w1(1, 0, "mid0")
         w2_raw = held([P, H_PASSES, 2 * H], U8, "w2_raw", tag="mid0")
@@ -221,16 +236,20 @@ def tile_list_perfusion_viability_scores_kernel(
         load_flow(1)
         quantize_w1(1, 2, "hold_a")
         for s in range(PACK, SLICES):
-            first_product(s)
+            first_product(s, s, whole)
 
-        x23 = held([P, 2, S], F32, "x23", tag="hold_a")
-        for s in (2, 3):
-            put(s)
-            pick(s, x23[:, s - 2, :])
-        for s in range(PACK):
-            difference(s, whole)
+        def step(s):
+            pick(s, "row%d" % (s + 2) if s + 2 < SLICES else "row0")
+            difference(s, whole, nc.gpsimd)
+            if s + 2 < SLICES:
+                put(s + 2)
+            if s + 3 < SLICES:
+                gain(s + 3, nc.gpsimd, "row%d" % (s + 2))
             activate(s, whole)
             residual(s, whole)
+
+        for s in range(PACK):
+            step(s)
 
         w2_codes = held([P, H_PASSES, 2 * H], U8, "w2_codes")
         nc.scalar.copy(
@@ -266,33 +285,23 @@ def tile_list_perfusion_viability_scores_kernel(
             weave(nc.scalar.copy, w3_staged[:, b * PACK * N : (b + 1) * PACK * N], w3_raw[:, b])
         w3_codes, w3_plane = quantize("w3", w3_staged[:], H_PASSES * N)
 
-        put(4)
-        pick(4, held([P, S], F32, "x4", tag="hold_w3")[:])
-        difference(4, whole)
         for c in range(CHUNKS):
             quantize_z(0, c, nc.scalar.copy)
             second_product(0, c)
-        activate(4, whole)
-        residual(4, whole)
-        for s in (5, 6):
-            put(s)
-            pick(s, held([P, S], F32, "x%d" % s, tag="hold_z0%d" % (s - 5))[:])
-            difference(s, whole)
-            activate(s, whole)
-            residual(s, whole)
+        for s in range(PACK, SLICES - 1):
+            step(s)
 
         last = SLICES - 1
-        put(last)
-        x[last] = ring_x(last)
+        x[last] = held([P, S], F32, "x_last", tag="row1")
         for c in range(CHUNKS):
             cols = chunk_cols[c]
             nc.vector.tensor_tensor(
                 x[last][:, cols],
-                pages[last % PAGES][:].indirect(list3[:, c * CW // 16 : (c + 1) * CW // 16]),
+                pages[last % PAGES][:].indirect(list3[:, chunk_entries[c]]),
                 wgt_sb[:, cols],
                 ALU.mult,
             )
-            difference(last, cols)
+            difference(last, cols, nc.vector)
             d = flow_sb[1][:, PACK - 1, cols]
             act = ring.tile([P, CW], F32, name="act_last%d" % c, tag="act", bufs=2)
             nc.scalar.activation(act[:], d, ACT.Gelu_apprx_tanh)

@@ -94,7 +94,7 @@ def tile_list_perfusion_viability_scores_kernel(
         def round_w1(b, a, staged):
             dealt = staged.rearrange("p (i m t) -> p m t i", i=PACK, t=PACK)
             rows = w1_raw[b, a][:].rearrange("p t (m i) -> p m t i", i=PACK)
-            if b == 0:
+            if (b, a) == (0, K_PASSES - 1):
                 nc.scalar.copy(out=dealt[:, : P // 2], in_=rows[:, : P // 2])
                 nc.vector.tensor_copy(out=dealt[:, P // 2 :], in_=rows[:, P // 2 :])
             else:
@@ -117,6 +117,11 @@ def tile_list_perfusion_viability_scores_kernel(
             round_w1(b, a, staged[:])
             w1_codes[b, a], w1_planes[b, a] = quantize("w1_%d%d" % (b, a), staged[:], K_PASS)
 
+        w2_planes = held([P, H_PASSES, H], U8, "w2_planes")
+        nc.vector.tensor_copy(
+            out=w2_planes[:].rearrange("p a (b i m) -> p (a b) i m", i=PACK, m=P),
+            in_=w2_planes_raw[:].rearrange("p a (b m i) -> p (a b) i m", i=PACK, m=P),
+        )
         quantize_w1(0, 0, "mid0")
         load_tab(1)
         quantize_w1(0, 1, "mid1")
@@ -131,11 +136,6 @@ def tile_list_perfusion_viability_scores_kernel(
         nc.sync.dma_start(out=gsum_sb, in_=gsum.rearrange("(b p i) -> p b i", p=P, i=PACK))
         nc.vector.tensor_copy(v_planes[:], tab_planes[:].indirect(list1[:]))
         quantize_w1(0, 2, "mid3")
-        w2_planes = held([P, H_PASSES, H], U8, "w2_planes", tag="mid3")
-        nc.vector.tensor_copy(
-            out=w2_planes[:].rearrange("p a (b i m) -> p (a b) i m", i=PACK, m=P),
-            in_=w2_planes_raw[:].rearrange("p a (b m i) -> p (a b) i m", i=PACK, m=P),
-        )
         load_w1(1, 0)
         look_up(0)
         load_w1(1, 1)

from contextlib import ExitStack

import concourse.mybir as mybir

K, H, N, T, S, T2 = 1536, 1024, 256, 2048, 512, 1024
FLOPS = 2 * K * H * S + 2 * H * H * S + 2 * H * N * S

F32 = mybir.dt.float32
BF16 = mybir.dt.bfloat16
I32 = mybir.dt.int32
U32 = mybir.dt.uint32
U16 = mybir.dt.uint16
U8 = mybir.dt.uint8
FP8X4 = mybir.dt.float8_e4m3fn_x4
FP4X4 = mybir.dt.float4_e2m1fn_x4
ACT = mybir.ActivationFunctionType
ALU = mybir.AluOpType

P = 128
PACK = 4
K_PASS = P * PACK
K_PASSES = K // K_PASS
H_PASSES = H // K_PASS
SLICES = H // P
CHUNKS = 2
CW = S // CHUNKS
PAGES = 3


def tile_list_perfusion_viability_scores_kernel(
    tc, tab_words, tab_scales, offs, w1, offs2, wgs, offs3, wgt, flow, gact, w2_words, w2_scales, gsum, w3, out
):
    nc = tc.nc
    with ExitStack() as ctx:
        keep = ctx.enter_context(tc.tile_pool(name="keep", bufs=1))
        ring = ctx.enter_context(tc.tile_pool(name="ring", bufs=3))
        psum = ctx.enter_context(tc.psum_pool(name="psum", bufs=1))

        def held(shape, dtype, name, tag=""):
            return keep.tile(shape, dtype, name=name, tag=tag or name, align_bytes=64)

        def bank(k, shape, name):
            return psum.tile(shape, F32, name=name, tag="bank%d" % k)

        whole = slice(0, S)
        chunk_cols = [slice(c * CW, (c + 1) * CW) for c in range(CHUNKS)]
        chunk_entries = [slice(c * CW // 16, (c + 1) * CW // 16) for c in range(CHUNKS)]

        list1 = held([P, S // 16], U16, "list1")
        list2 = held([P, S // 16], U16, "list2")
        list3 = held([P, S // 16], U16, "list3")
        tab_planes = held([P, T], U8, "tab_planes")
        w2_planes_raw = held([P, H_PASSES, H], U8, "w2_planes_raw")
        nc.vector.memset(tab_planes[:].bitcast(I32), 0)
        nc.vector.memset(w2_planes_raw[:].rearrange("p a c -> p (a c)").bitcast(I32), 0)
        pages = [held([P, T2], F32, "page%d" % k) for k in range(PAGES)]
        for page in pages:
            nc.vector.memset(page[:], 0.0)
        for q in range(4):
            nc.gpsimd.dma_start(
                out=w2_planes_raw[32 * q : 32 * q + 4, :, :].bitcast(I32),
                in_=w2_scales[:, 4 * q : 4 * q + 4, :].rearrange("a r c -> r a c").bitcast(I32),
            )

        w1_slot = {(0, 0): 0, (0, 1): 1, (0, 2): 2, (1, 0): 2, (1, 1): 3, (1, 2): 0}
        tab_slot = [3, 0, 1]
        flow_slot = [1, 3]
        w1_raw, tab = {}, {}

        def load_w1(b, a):
            w1_raw[b, a] = held([P, PACK, K_PASS], F32, "w1_raw%d%d" % (b, a), tag="big%d" % w1_slot[b, a])
            rows = w1[a * K_PASS : (a + 1) * K_PASS, b * K_PASS : (b + 1) * K_PASS]
            nc.sync.dma_start(out=w1_raw[b, a][:], in_=rows.rearrange("(p t) c -> p t c", t=PACK))

        def load_tab(a):
            tab[a] = held([P, T], I32, "tab%d" % a, tag="big%d" % tab_slot[a])
            nc.sync.dma_start(out=tab[a][:], in_=tab_words[a].rearrange("p t i -> p (t i)").bitcast(I32))

        load_w1(0, 0)
        nc.sync.dma_start(list1[:], offs)
        nc.sync.dma_start(list2[:], offs2)
        nc.sync.dma_start(list3[:], offs3)
        load_w1(0, 1)
        load_w1(0, 2)
        load_tab(0)
        for q in range(4):
            nc.sync.dma_start(
                out=tab_planes[32 * q : 32 * q + 4 * K_PASSES, :].bitcast(I32),
                in_=tab_scales[:, 4 * q : 4 * q + 4, :].bitcast(I32),
            )

        w1_codes, w1_planes = {}, {}

        def round_w1(b, a, staged):
            dealt = staged.rearrange("p (i m t) -> p m t i", i=PACK, t=PACK)
            rows = w1_raw[b, a][:].rearrange("p t (m i) -> p m t i", i=PACK)
            if (b, a) == (0, K_PASSES - 1):
                nc.scalar.copy(out=dealt[:, : P // 2], in_=rows[:, : P // 2])
                nc.vector.tensor_copy(out=dealt[:, P // 2 :], in_=rows[:, P // 2 :])
            else:
                nc.scalar.copy(out=dealt, in_=rows)

        def quantize(name, staged, words):
            codes = held([P, words], U32, name + "_codes")
            plane = held([P, words], U8, name + "_plane")
            nc.vector.quantize_mx(out=codes[:].bitcast(FP8X4), scales=plane[:], in_=staged)
            return codes, plane

        v_words = [held([P, S], U32, "v_words%d" % a) for a in range(K_PASSES)]
        v_planes = held([P, S], U8, "v_planes")

        def look_up(a):
            nc.vector.tensor_copy(v_words[a][:], tab[a][:].bitcast(U32).indirect(list1[:]))

        def quantize_w1(b, a, tag):
            staged = held([P, PACK * K_PASS], BF16, "staged%d%d" % (b, a), tag=tag)
            round_w1(b, a, staged[:])
            w1_codes[b, a], w1_planes[b, a] = quantize("w1_%d%d" % (b, a), staged[:], K_PASS)

        w2_planes = held([P, H_PASSES, H], U8, "w2_planes")
        nc.vector.tensor_copy(
            out=w2_planes[:].rearrange("p a (b i m) -> p (a b) i m", i=PACK, m=P),
            in_=w2_planes_raw[:].rearrange("p a (b m i) -> p (a b) i m", i=PACK, m=P),
        )
        quantize_w1(0, 0, "mid0")
        load_tab(1)
        quantize_w1(0, 1, "mid1")
        load_tab(2)
        gains = held([P, 2 * S + 2 * SLICES], F32, "gains", tag="mid1")
        wgs_sb, wgt_sb = gains[:, :S], gains[:, S : 2 * S]
        gact_sb = gains[:, 2 * S : 2 * S + SLICES].rearrange("p (b i) -> p b i", i=PACK)
        gsum_sb = gains[:, 2 * S + SLICES :].rearrange("p (b i) -> p b i", i=PACK)
        nc.sync.dma_start(out=wgs_sb, in_=wgs)
        nc.sync.dma_start(out=wgt_sb, in_=wgt)
        nc.sync.dma_start(out=gact_sb, in_=gact.rearrange("(b p i) -> p b i", p=P, i=PACK))
        nc.sync.dma_start(out=gsum_sb, in_=gsum.rearrange("(b p i) -> p b i", p=P, i=PACK))
        nc.vector.tensor_copy(v_planes[:], tab_planes[:].indirect(list1[:]))
        quantize_w1(0, 2, "mid3")
        load_w1(1, 0)
        look_up(0)
        load_w1(1, 1)
        look_up(1)
        load_w1(1, 2)
        for c in range(CHUNKS):
            nc.vector.tensor_copy(
                v_words[2][:, chunk_cols[c]], tab[2][:].bitcast(U32).indirect(list1[:, chunk_entries[c]])
            )
        flow_sb = {}

        def load_flow(b):
            flow_sb[b] = held([P, PACK, S], F32, "flow%d" % b, tag="big%d" % flow_slot[b])
            nc.sync.dma_start(out=flow_sb[b][:], in_=flow.rearrange("(b p i) j -> b p i j", p=P, i=PACK)[b])

        load_flow(0)

        h = {s: held([P, S], F32, "h%d" % s, tag="row%d" % s) for s in range(SLICES)}

        def first_product(s, k, cols):
            b, i = divmod(s, PACK)
            acc = bank(k, [P, cols.stop - cols.start], "h_acc%d_%d" % (s, cols.start))
            w_cols = slice(i * P, (i + 1) * P)
            for a in range(K_PASSES):
                nc.tensor.matmul_mx(
                    out=acc[:],
                    lhsT=w1_codes[b, a][:, w_cols].bitcast(FP8X4),
                    lhsT_scale=w1_planes[b, a][:, w_cols],
                    rhs=v_words[a][:, cols].bitcast(FP8X4),
                    rhs_scale=v_planes[4 * a : P, cols],
                    start=(a == 0),
                    stop=(a == K_PASSES - 1),
                )
            nc.scalar.activation(h[s][:, cols], acc[:], ACT.Abs)

        for c in range(CHUNKS):
            first_product(0, c, chunk_cols[c])
        for s in range(1, PACK):
            first_product(s, (s - 1) % 2, whole)

        x, gained = {}, {}

        def gain(s, engine, tag):
            gained[s] = held([P, S], F32, "gained%d" % s, tag=tag)
            engine.tensor_tensor(gained[s][:], h[s][:], wgs_sb, ALU.mult)

        def put(s):
            nc.vector.tensor_copy(pages[s % PAGES][:].indirect(list2[:]), gained[s][:])

        def pick(s, tag):
            x[s] = held([P, S], F32, "x%d" % s, tag=tag)
            nc.vector.tensor_tensor(x[s][:], pages[s % PAGES][:].indirect(list3[:]), wgt_sb, ALU.mult)

        z16 = [held([P, PACK, S], BF16, "z16_%d" % b) for b in range(H_PASSES)]

        def difference(s, cols, engine):
            b, i = divmod(s, PACK)
            d = flow_sb[b][:, i, cols]
            engine.tensor_tensor(d, x[s][:, cols], d, ALU.subtract)

        def activate(s, cols):
            b, i = divmod(s, PACK)
            d = flow_sb[b][:, i, cols]
            act = ring.tile([P, S], F32, name="act%d_%d" % (s, cols.start), tag="act", bufs=2)
            nc.scalar.activation(act[:, cols], d, ACT.Gelu_apprx_tanh)
            nc.scalar.activation(z16[b][:, i, cols], act[:, cols], ACT.Copy, scale=gact_sb[:, b, i : i + 1])

        def residual(s, cols):
            b, i = divmod(s, PACK)
            d = flow_sb[b][:, i, cols]
            nc.scalar.activation(d, d, ACT.Copy, scale=gsum_sb[:, b, i : i + 1])

        def weave(engine_copy, dst, rows):
            engine_copy(
                out=dst.rearrange("p (c u t) -> p c t u", u=PACK, t=PACK),
                in_=rows.rearrange("p t (c u) -> p c t u", u=PACK),
            )


        for c in range(CHUNKS):
            cols = chunk_cols[c]
            nc.vector.tensor_tensor(
                pages[0][:].indirect(list2[:, chunk_entries[c]]), h[0][:, cols], wgs_sb[:, cols], ALU.mult
            )
        gain(1, nc.vector, "gained1")
        put(1)
        gain(2, nc.gpsimd, "row1")

        quantize_w1(1, 0, "mid0")
        w2_raw = held([P, H_PASSES, 2 * H], U8, "w2_raw", tag="mid0")
        nc.sync.dma_start(out=w2_raw[:].bitcast(I32), in_=w2_words.rearrange("a p c -> p a c").bitcast(I32))
        w3_raw = held([P, H_PASSES, PACK, N], F32, "w3_raw", tag="big2")
        for b in range(H_PASSES):
            nc.sync.dma_start(
                out=w3_raw[:, b], in_=w3[b * K_PASS : (b + 1) * K_PASS, :].rearrange("(p t) n -> p t n", t=PACK)
            )
        quantize_w1(1, 1, "mid2")
        load_flow(1)
        quantize_w1(1, 2, "hold_a")
        for s in range(PACK, SLICES):
            first_product(s, s, whole)

        def step(s):
            pick(s, "row%d" % (s + 2) if s + 2 < SLICES else "row0")
            difference(s, whole, nc.gpsimd)
            if s + 2 < SLICES:
                put(s + 2)
            if s + 3 < SLICES:
                gain(s + 3, nc.gpsimd, "row%d" % (s + 2))
            activate(s, whole)
            residual(s, whole)

        for s in range(PACK):
            step(s)

        w2_codes = held([P, H_PASSES, 2 * H], U8, "w2_codes")
        nc.scalar.copy(
            out=w2_codes[:].bitcast(U16).rearrange("p a (b i m) -> p (a b) i m", i=PACK, m=P),
            in_=w2_raw[:].bitcast(U16).rearrange("p a (b m i) -> p (a b) i m", i=PACK, m=P),
        )

        z_codes, z_planes, acc2 = {}, {}, {}

        def quantize_z(b, c, engine_copy):
            woven = held([P, PACK * CW], BF16, "z_woven%d%d" % (b, c), tag="hold_z%d%d" % (b, c))
            weave(engine_copy, woven[:], z16[b][:, :, chunk_cols[c]])
            z_codes[b, c], z_planes[b, c] = quantize("z%d%d" % (b, c), woven[:], CW)

        def second_product(a, c):
            for u in range(SLICES // 2):
                if a == 0:
                    acc2[c, u] = bank(PACK * c + u, [P, 2, CW], "acc2_%d%d" % (c, u))
                for e in range(2):
                    s = 2 * u + e
                    nc.tensor.matmul_mx(
                        out=acc2[c, u][:, e, :],
                        lhsT=w2_codes[:, a, 2 * P * s : 2 * P * (s + 1)].bitcast(FP4X4),
                        lhsT_scale=w2_planes[:, a, P * s : P * (s + 1)],
                        rhs=z_codes[a, c][:].bitcast(FP8X4),
                        rhs_scale=z_planes[a, c][:],
                        start=(a == 0 and e == 0),
                        stop=(a == H_PASSES - 1 and e == 1),
                    )

        w3_staged = held([P, H_PASSES * PACK * N], BF16, "w3_staged", tag="hold_w3")
        for b in range(H_PASSES):
            weave(nc.scalar.copy, w3_staged[:, b * PACK * N : (b + 1) * PACK * N], w3_raw[:, b])
        w3_codes, w3_plane = quantize("w3", w3_staged[:], H_PASSES * N)

        for c in range(CHUNKS):
            quantize_z(0, c, nc.scalar.copy)
            second_product(0, c)
        for s in range(PACK, SLICES - 1):
            step(s)

        last = SLICES - 1
        x[last] = held([P, S], F32, "x_last", tag="row1")
        for c in range(CHUNKS):
            cols = chunk_cols[c]
            nc.vector.tensor_tensor(
                x[last][:, cols],
                pages[last % PAGES][:].indirect(list3[:, chunk_entries[c]]),
                wgt_sb[:, cols],
                ALU.mult,
            )
            difference(last, cols, nc.vector)
            d = flow_sb[1][:, PACK - 1, cols]
            act = ring.tile([P, CW], F32, name="act_last%d" % c, tag="act", bufs=2)
            nc.scalar.activation(act[:], d, ACT.Gelu_apprx_tanh)
            nc.vector.tensor_scalar_mul(z16[1][:, PACK - 1, cols], act[:], gact_sb[:, 1, PACK - 1 : PACK])
            quantize_z(1, c, nc.vector.tensor_copy)
            second_product(1, c)
            residual(last, cols)

        resp = {}
        for c in range(CHUNKS):
            for u in range(SLICES // 2):
                resp[c, u] = ring.tile([P, 2, CW], F32, name="resp%d%d" % (c, u), tag="resp", bufs=6)
                nc.scalar.activation(resp[c, u][:], acc2[c, u][:], ACT.Tanh)

        for c in range(CHUNKS):
            cols = chunk_cols[c]
            y_codes, y_planes = {}, {}
            for b in range(H_PASSES):
                y16 = ring.tile([P, PACK, CW], BF16, name="y16_%d%d" % (c, b), tag="y16")
                for i in range(PACK):
                    nc.vector.scalar_tensor_tensor(
                        y16[:, i, :], resp[c, 2 * b + i // 2][:, i % 2, :], gsum_sb[:, b, i : i + 1],
                        flow_sb[b][:, i, cols], ALU.mult, ALU.add,
                    )
                woven = ring.tile([P, PACK * CW], BF16, name="y_woven%d%d" % (c, b), tag="y_woven", align_bytes=64)
                weave(nc.scalar.copy if b == 0 else nc.vector.tensor_copy, woven[:], y16[:])
                y_codes[b], y_planes[b] = quantize("y%d%d" % (c, b), woven[:], CW)
            acc3 = bank(c, [P, N // P, CW], "acc3_%d" % c)
            for b in range(H_PASSES):
                for nt in range(N // P):
                    w_cols = slice(b * N + nt * P, b * N + (nt + 1) * P)
                    nc.tensor.matmul_mx(
                        out=acc3[:, nt, :],
                        lhsT=w3_codes[:, w_cols].bitcast(FP8X4),
                        lhsT_scale=w3_plane[:, w_cols],
                        rhs=y_codes[b][:].bitcast(FP8X4),
                        rhs_scale=y_planes[b][:],
                        start=(b == 0 and nt == 0),
                        stop=(b == H_PASSES - 1 and nt == N // P - 1),
                    )
            result = ring.tile([P, N // P, CW], F32, name="result%d" % c, tag="result", bufs=2)
            nc.scalar.copy(out=result[:], in_=acc3[:])
            nc.sync.dma_start(out=out[:, cols].rearrange("(nt p) j -> p nt j", p=P), in_=result[:])
